import numpy as np
import ml_dtypes


def mxq(x, axis, fmt="e4m3"):
    dtype, down = {"e4m3": (ml_dtypes.float8_e4m3fn, 7), "e5m2": (ml_dtypes.float8_e5m2, 14)}[fmt]
    v = np.moveaxis(np.asarray(x, np.float32).astype(ml_dtypes.bfloat16).astype(np.float64), axis, -1)
    blocks = v.reshape(v.shape[:-1] + (-1, 32))
    amax = np.abs(blocks).max(-1, keepdims=True)
    byte = np.maximum(np.where(amax > 0, np.frexp(amax)[1] - 1 + 127, 0) - down, 1)
    scale = np.exp2(byte - 127.0)
    codes = (blocks / scale).astype(np.float32).astype(dtype).astype(np.float64)
    return np.moveaxis((codes * scale).reshape(v.shape), -1, axis)


WIDE = False


def mx_kscale(k):
    if not WIDE:
        return np.ones(k)
    levels = np.array([10, -10, 5, -5, 0])
    if k % 512:
        return np.exp2(np.random.permutation(np.resize(levels, k // 32))).repeat(32)
    a = np.empty((k // 512, 16))
    for p in range(k // 512):
        a[p, :8] = np.random.permutation(np.resize(levels, 8))
        for g in range(8):
            far = levels[np.abs(levels - a[p, g]) >= 10]
            a[p, g + 8] = far[np.random.randint(len(far))]
    return np.exp2(a.ravel()).repeat(32)


def f64(x):
    return np.asarray(x).astype(np.float64)


def striped(idx):
    return np.tile(idx.reshape(-1, 16).T, (8, 1)).astype(np.uint16)


def unstriped(offs):
    return offs[:16].T.reshape(-1).astype(np.int64)


def gelu(v):
    return 0.5 * v * (1.0 + np.tanh(np.sqrt(2.0 / np.pi) * (v + 0.044715 * v**3)))


K, T, E, C, H, N = 1024, 512, 4, 256, 1024, 256


def by_expert(wq, xq):
    return np.concatenate([wq[e].T @ xq[:, e * C:(e + 1) * C] for e in range(E)], axis=1)


def setup_inputs():
    n = np.random.standard_normal
    s = mx_kscale(K)[:, None]
    u = mx_kscale(H)
    first = np.random.permutation(np.repeat(np.arange(E), T // E))
    second = (first + 1 + np.random.permutation(np.repeat(np.arange(E - 1), -(-T // (E - 1)))[:T])) % E
    while np.bincount(second, minlength=E).max() != T // E:
        load = np.bincount(second, minlength=E); hi, lo = int(load.argmax()), int(load.argmin())
        t = np.flatnonzero((second == hi) & (first != lo))[0]; second[t] = lo
    slot_token = np.empty(E * C, np.int64); pos = np.empty((2, T), np.int64); fill = np.zeros(E, np.int64)
    place = np.stack([np.random.permutation(C) for _ in range(E)])
    for r, deal in enumerate((first, second)):
        for t in np.random.permutation(T):
            e = deal[t]; j = e * C + place[e, fill[e]]; fill[e] += 1; slot_token[j] = t; pos[r, t] = j
    g = np.random.uniform(0.2, 0.8, T)
    return {
        "xT": (n((K, T)) * s).astype(np.float32),
        "w1": (n((E, K, H)) / np.sqrt(K) / s[None] * u[None, None, :]).astype(np.float32),
        "w2": (n((E, H, N)) / np.sqrt(H) / u[None, :, None]).astype(np.float32),
        "gate": np.stack([np.tile(g, (N, 1)), np.tile(1.0 - g, (N, 1))]).astype(np.float32),
        "offs": striped(slot_token),
        "pos1": striped(pos[0]),
        "pos2": striped(pos[1]),
    }


def reference(xT, w1, w2, gate, offs, pos1, pos2):
    idx = unstriped(offs)
    xq = mxq(f64(xT)[:, idx], 0, "e4m3")
    h = gelu(by_expert(mxq(f64(w1), 1, "e4m3"), xq))
    y = by_expert(mxq(f64(w2), 1, "e4m3"), mxq(h, 0, "e4m3"))
    return f64(gate[0]) * y[:, unstriped(pos1)] + f64(gate[1]) * y[:, unstriped(pos2)]

@@ -1,0 +1,295 @@
+from contextlib import ExitStack
+
+import concourse.mybir as mybir
+
+K, T, E, C, H, N = 1024, 512, 4, 256, 1024, 256
+FLOPS = 2 * E * C * (K * H + H * N)
+
+F32 = mybir.dt.float32
+BF16 = mybir.dt.bfloat16
+I32 = mybir.dt.int32
+U32 = mybir.dt.uint32
+U16 = mybir.dt.uint16
+U8 = mybir.dt.uint8
+FP8X4 = mybir.dt.float8_e4m3fn_x4
+GELU = mybir.ActivationFunctionType.Gelu_apprx_tanh
+MULT = mybir.AluOpType.mult
+ADD = mybir.AluOpType.add
+
+P = 128
+CHUNK = 2048
+SLOT = 2 * CHUNK
+DEPTH = 6
+ORDER = ["x0","x1","w00","w01","w10","w11","w20","w21","w30","w31","h0","h1","h2","h3","gate"]
+X_ENGINE = "vs"
+W1_ENGINE = "sssvvvsvvvsvvvss"
+W2_ENGINE = "vvvsvvsv"
+Y_ENGINE = "ssssssvs"
+IN_HALVES = [2,3]
+
+
+def tile_routed_moe_kernel(tc, xT, w1, w2, gate, offs, pos1, pos2, out):
+    nc = tc.nc
+    with ExitStack() as ctx:
+        lists = ctx.enter_context(tc.tile_pool(name="lists", bufs=1))
+        keep = ctx.enter_context(tc.tile_pool(name="keep", bufs=1))
+        stage = ctx.enter_context(tc.tile_pool(name="stage", bufs=DEPTH))
+        grp = ctx.enter_context(tc.tile_pool(name="grp", bufs=4))
+        hid = ctx.enter_context(tc.tile_pool(name="hid", bufs=3))
+        fin = ctx.enter_context(tc.tile_pool(name="fin", bufs=2))
+        ps1 = ctx.enter_context(tc.psum_pool(name="ps1", bufs=4))
+        ps2 = ctx.enter_context(tc.psum_pool(name="ps2", bufs=4))
+
+        offs_t = lists.tile([P, E * C // 16], U16, name="offs_t")
+        pos1_t = lists.tile([P, T // 16], U16, name="pos1_t")
+        pos2_t = lists.tile([P, T // 16], U16, name="pos2_t")
+        nc.sync.dma_start(offs_t[:], offs)
+
+        xT_v = xT.rearrange("(s p j) t -> s p j t", p=P, j=4)
+        w1_v = w1.rearrange("e (s p j) h -> e s p j h", p=P, j=4)
+        w2_v = w2.rearrange("e (g p j) n -> p e g (j n)", p=P, j=4)
+        gate_v = gate.rearrange("r (b p) t -> p r b t", p=P)
+
+        issued = [0]
+        reads = {}
+        raws = {}
+
+        def readers_of(name):
+            return 1 if name[0] == "x" else 2
+
+        def load():
+            i = issued[0]
+            if i >= len(ORDER):
+                return False
+            if i >= DEPTH and reads.get(ORDER[i - DEPTH], 0) < readers_of(ORDER[i - DEPTH]):
+                return False
+            name = ORDER[i]
+            issued[0] += 1
+            dma = nc.sync.dma_start
+            width = SLOT if name[0] == "w" else CHUNK
+            raw = stage.tile([P, width], F32, name="raw", tag="raw")
+            if name[0] == "x":
+                dma(out=raw[:].rearrange("p (j t) -> p j t", j=4), in_=xT_v[int(name[1])])
+            elif name[0] == "w":
+                dma(out=raw[:].rearrange("p (j h) -> p j h", j=4), in_=w1_v[int(name[1]), int(name[2])])
+            elif name[0] == "h":
+                e = int(name[1])
+                if e in IN_HALVES:
+                    for g in range(2):
+                        dma(out=raw[:, g * 1024 : (g + 1) * 1024], in_=w2_v[:, e, g])
+                else:
+                    dma(out=raw[:].rearrange("p (g c) -> p g c", g=2), in_=w2_v[:, e])
+            else:
+                dma(out=raw[:].rearrange("p (r b t) -> p r b t", r=2, b=2), in_=gate_v)
+            raws[name] = raw
+            return True
+
+        def pump():
+            while load():
+                pass
+
+        def was_read(name):
+            reads[name] = reads.get(name, 0) + 1
+            pump()
+
+        def copy_on(eng, dst, src):
+            if eng == "v":
+                nc.vector.tensor_copy(out=dst, in_=src)
+            else:
+                nc.scalar.copy(out=dst, in_=src)
+
+        def interleave(eng, dst, src):
+            copy_on(
+                eng,
+                dst.rearrange("p (c i j) -> p c j i", i=4, j=4),
+                src.rearrange("p (j c i) -> p c j i", j=4, i=4),
+            )
+
+        def interleave_permuted(eng, dst, src):
+            if eng == "v":
+                nc.vector.tensor_copy(
+                    out=dst.rearrange("p (u v m j) -> p u m j v", u=2, v=2, j=4),
+                    in_=src.rearrange("p j (m u v) -> p u m j v", u=2, v=2),
+                )
+            else:
+                nc.scalar.copy(
+                    out=dst.rearrange("p (t m j) -> p m j t", t=4, j=4),
+                    in_=src.rearrange("p j (m t) -> p m j t", t=4),
+                )
+
+        pump()
+        warm = keep.tile([P, 1], F32, name="warm")
+        warm2 = keep.tile([P, 1], F32, name="warm2")
+        nc.vector.memset(warm[:], 0.0)
+        nc.scalar.activation(out=warm2[:], in_=warm[:], func=GELU)
+
+        xw = [keep.tile([P, 2 * T], I32, name="xw%d" % s, align_bytes=64) for s in range(2)]
+        xs = [keep.tile([P, 2 * T], U8, name="xs%d" % s, align_bytes=64) for s in range(2)]
+        for s in range(2):
+            nc.vector.memset(xw[s][:, T : 2 * T], 0)
+            nc.gpsimd.memset(xs[s][:], 0)
+
+        gw = {}
+        gs = {}
+
+        def gather(first, count):
+            sl = offs_t[:, first * (C // 16) : (first + count) * (C // 16)]
+            for s in range(2):
+                words = keep.tile([P, count * C], U32, name="gw%d_%d" % (s, first), align_bytes=64)
+                scales = keep.tile([P, count * C], U8, name="gs%d_%d" % (s, first), align_bytes=64)
+                nc.vector.tensor_copy(out=words[:], in_=xw[s][:].bitcast(U32).indirect(sl))
+                nc.vector.tensor_copy(out=scales[:], in_=xs[s][:].indirect(sl))
+                for e in range(first, first + count):
+                    part = slice((e - first) * C, (e - first + 1) * C)
+                    gw[(s, e)] = words[:, part]
+                    gs[(s, e)] = scales[:, part]
+
+        w1c = {}
+        w1s = {}
+        wgs = {}
+        hbs = {}
+        hc = {}
+        hs = {}
+
+        def w1_copy(e, s, g):
+            wg = grp.tile([P, CHUNK], BF16, name="wg", tag="grp", align_bytes=64)
+            name = "w%d%d" % (e, s)
+            src = raws[name][:].rearrange("p (j h) -> p j h", j=4)[:, :, g * 512 : (g + 1) * 512]
+            interleave_permuted(W1_ENGINE[4 * e + 2 * s + g], wg[:], src)
+            wgs[(e, s, g)] = wg
+            was_read(name)
+
+        def w1_quant(e, s, g):
+            c = (e, s, g)
+            w1c[c] = keep.tile([P, 512], U32, name="w1c%d%d%d" % c, align_bytes=64)
+            w1s[c] = keep.tile([P, 512], U8, name="w1s%d%d%d" % c, align_bytes=64)
+            nc.vector.quantize_mx(out=w1c[c][:].bitcast(FP8X4), scales=w1s[c][:], in_=wgs[c][:])
+
+        def layer1(e, g):
+            hb = hid.tile([P, 4 * C], BF16, name="hb", tag="hb", align_bytes=64)
+            hbs[2 * e + g] = hb
+            for half in range(2):
+                cols = slice(half * 128, (half + 1) * 128)
+                acc = ps1.tile([P, 4, 128], F32, name="acc1", tag="acc1")
+                for t in range(4):
+                    wcols = slice(t * 128, (t + 1) * 128)
+                    for s in range(2):
+                        nc.tensor.matmul_mx(
+                            out=acc[:, t, :],
+                            lhsT=w1c[(e, s, g)][:, wcols].bitcast(FP8X4),
+                            lhsT_scale=w1s[(e, s, g)][:, wcols],
+                            rhs=gw[(s, e)][:, cols].bitcast(FP8X4),
+                            rhs_scale=gs[(s, e)][:, cols],
+                            start=(s == 0),
+                            stop=(s == 1),
+                        )
+                nc.scalar.activation(
+                    out=hb[:, half * 512 : (half + 1) * 512].rearrange("p (n t) -> p n t", t=4),
+                    in_=acc[:].rearrange("p t n -> p n t"),
+                    func=GELU,
+                )
+
+        def h_quant(k):
+            hc[k] = keep.tile([P, C], U32, name="hc%d" % k, align_bytes=64)
+            hs[k] = keep.tile([P, C], U8, name="hs%d" % k, align_bytes=64)
+            nc.vector.quantize_mx(out=hc[k][:].bitcast(FP8X4), scales=hs[k][:], in_=hbs[k][:])
+
+        y = [keep.tile([P, E * C], F32, name="y%d" % b) for b in range(2)]
+        w2g = {}
+        w2c = {}
+        w2s = {}
+
+        def w2_copy(e, g):
+            wg = grp.tile([P, CHUNK // 2], BF16, name="wg2", tag="grp", align_bytes=64)
+            interleave(W2_ENGINE[2 * e + g], wg[:], raws["h%d" % e][:, g * 1024 : (g + 1) * 1024])
+            w2g[2 * e + g] = wg
+            was_read("h%d" % e)
+
+        def w2_quant(h):
+            w2c[h] = keep.tile([P, N], U32, name="w2c%d" % h, align_bytes=64)
+            w2s[h] = keep.tile([P, N], U8, name="w2s%d" % h, align_bytes=64)
+            nc.vector.quantize_mx(out=w2c[h][:].bitcast(FP8X4), scales=w2s[h][:], in_=w2g[h][:])
+
+        def layer2(e):
+            accs = []
+            for b in range(2):
+                acc = ps2.tile([P, C], F32, name="acc2", tag="acc2")
+                accs.append(acc)
+                wcols = slice(b * 128, (b + 1) * 128)
+                for g in range(2):
+                    nc.tensor.matmul_mx(
+                        out=acc[:],
+                        lhsT=w2c[2 * e + g][:, wcols].bitcast(FP8X4),
+                        lhsT_scale=w2s[2 * e + g][:, wcols],
+                        rhs=hc[2 * e + g][:].bitcast(FP8X4),
+                        rhs_scale=hs[2 * e + g][:],
+                        start=(g == 0),
+                        stop=(g == 1),
+                    )
+            for b in range(2):
+                copy_on(Y_ENGINE[2 * e + b], y[b][:, e * C : (e + 1) * C], accs[b][:])
+
+        pending = []
+        done2 = []
+
+        def second_layers():
+            for e in range(E):
+                if e not in done2 and 2 * e + 1 in w2c and 2 * e + 1 in hc:
+                    layer2(e)
+                    done2.append(e)
+
+        def hidden_quants():
+            for k in pending:
+                h_quant(k)
+            pending.clear()
+            second_layers()
+
+        xgs = []
+        for name in ORDER:
+            if name[0] == "x":
+                s = int(name[1])
+                xg = grp.tile([P, CHUNK], BF16, name="xg", tag="grp", align_bytes=64)
+                interleave(X_ENGINE[s], xg[:], raws[name][:])
+                was_read(name)
+                xgs.append(xg)
+                if s == 1:
+                    for i in range(2):
+                        nc.vector.quantize_mx(out=xw[i][:, 0:T].bitcast(FP8X4), scales=xs[i][:, 0:T], in_=xgs[i][:])
+                    gather(0, 1)
+            elif name[0] == "w":
+                e, s = int(name[1]), int(name[2])
+                for g in range(2):
+                    w1_copy(e, s, g)
+                if name == "w00":
+                    gather(1, 3)
+                if name == "w10":
+                    nc.sync.dma_start(pos1_t[:], pos1)
+                    nc.sync.dma_start(pos2_t[:], pos2)
+                for g in range(2):
+                    w1_quant(e, s, g)
+                hidden_quants()
+                if s == 1:
+                    for g in range(2):
+                        layer1(e, g)
+                        pending.append(2 * e + g)
+            elif name[0] == "h":
+                e = int(name[1])
+                for g in range(2):
+                    w2_copy(e, g)
+                hidden_quants()
+                for g in range(2):
+                    w2_quant(2 * e + g)
+                second_layers()
+        hidden_quants()
+
+        graw = raws["gate"]
+        for b in range(2):
+            a1 = fin.tile([P, T], F32, name="a1", tag="a1")
+            a2 = fin.tile([P, T], F32, name="a2", tag="a2")
+            res = fin.tile([P, T], F32, name="res", tag="res")
+            nc.vector.tensor_tensor(out=a1[:], in0=y[b][:].indirect(pos1_t[:]), in1=graw[:, b * T : (b + 1) * T], op=MULT)
+            nc.vector.tensor_tensor(
+                out=a2[:], in0=y[b][:].indirect(pos2_t[:]), in1=graw[:, (2 + b) * T : (3 + b) * T], op=MULT
+            )
+            nc.vector.tensor_tensor(out=res[:], in0=a1[:], in1=a2[:], op=ADD)
+            nc.sync.dma_start(out=out[b * P : (b + 1) * P, :], in_=res[:])

@@ -124,25 +124,25 @@ def tile_routed_moe_kernel(tc, xT, w1, w2, gate, offs, pos1, pos2, out):
         nc.scalar.activation(out=warm2[:], in_=warm[:], func=GELU)
 
         xw = [keep.tile([P, 2 * T], I32, name="xw%d" % s, align_bytes=64) for s in range(2)]
-        xs = [keep.tile([P, 2 * T], U8, name="xs%d" % s, align_bytes=64) for s in range(2)]
+        xs = keep.tile([P, 2 * T], U8, name="xs", align_bytes=64)
         for s in range(2):
             nc.vector.memset(xw[s][:, T : 2 * T], 0)
-            nc.gpsimd.memset(xs[s][:], 0)
+        nc.gpsimd.memset(xs[:], 0)
 
         gw = {}
         gs = {}
 
         def gather(first, count):
             sl = offs_t[:, first * (C // 16) : (first + count) * (C // 16)]
+            scales = keep.tile([P, count * C], U8, name="gs_%d" % first, align_bytes=64)
+            nc.vector.tensor_copy(out=scales[:], in_=xs[:].indirect(sl))
             for s in range(2):
                 words = keep.tile([P, count * C], U32, name="gw%d_%d" % (s, first), align_bytes=64)
-                scales = keep.tile([P, count * C], U8, name="gs%d_%d" % (s, first), align_bytes=64)
                 nc.vector.tensor_copy(out=words[:], in_=xw[s][:].bitcast(U32).indirect(sl))
-                nc.vector.tensor_copy(out=scales[:], in_=xs[s][:].indirect(sl))
                 for e in range(first, first + count):
                     part = slice((e - first) * C, (e - first + 1) * C)
                     gw[(s, e)] = words[:, part]
-                    gs[(s, e)] = scales[:, part]
+                    gs[(s, e)] = scales[4 * s : P, part]
 
         w1c = {}
         w1s = {}
@@ -254,7 +254,7 @@ def tile_routed_moe_kernel(tc, xT, w1, w2, gate, offs, pos1, pos2, out):
                 xgs.append(xg)
                 if s == 1:
                     for i in range(2):
-                        nc.vector.quantize_mx(out=xw[i][:, 0:T].bitcast(FP8X4), scales=xs[i][:, 0:T], in_=xgs[i][:])
+                        nc.vector.quantize_mx(out=xw[i][:, 0:T].bitcast(FP8X4), scales=xs[4 * i : P, 0:T], in_=xgs[i][:])
                     gather(0, 1)
             elif name[0] == "w":
                 e, s = int(name[1]), int(name[2])

@@ -22,7 +22,7 @@ SLOT = 2 * CHUNK
 DEPTH = 6
 ORDER = ["x0","x1","w00","w01","w10","w11","w20","w21","w30","w31","h0","h1","h2","h3","gate"]
 X_ENGINE = "vs"
-W1_ENGINE = "sssvvvsvvvsvvvss"
+W1_ENGINE = "sssvvvsvvvsvvvvs"
 W2_ENGINE = "vvvsvvsv"
 Y_ENGINE = "ssssssvs"
 IN_HALVES = [2,3]

@@ -23,9 +23,10 @@ DEPTH = 6
 ORDER = ["x0","x1","w00","w01","w10","w11","w20","w21","w30","w31","h0","h1","h2","h3","gate"]
 X_ENGINE = "vs"
 W1_ENGINE = "sssvvvsvvvsvvvvs"
-W2_ENGINE = "vvvsvvsv"
+W2_ENGINE = "vvvsvvvv"
 Y_ENGINE = "ssssssvs"
-IN_HALVES = [2,3]
+IN_HALVES = [2]
+BY_BLOCK = [3]
 
 
 def tile_routed_moe_kernel(tc, xT, w1, w2, gate, offs, pos1, pos2, out):
@@ -201,7 +202,15 @@ def tile_routed_moe_kernel(tc, xT, w1, w2, gate, offs, pos1, pos2, out):
 
         def w2_copy(e, g):
             wg = grp.tile([P, CHUNK // 2], BF16, name="wg2", tag="grp", align_bytes=64)
-            interleave(W2_ENGINE[2 * e + g], wg[:], raws["h%d" % e][:, g * 1024 : (g + 1) * 1024])
+            if e in BY_BLOCK:
+                src = raws["h%d" % e][:].rearrange("p (q j n) -> p q j n", q=2, j=4)[:, :, :, g * 128 : (g + 1) * 128]
+                copy_on(
+                    W2_ENGINE[2 * e + g],
+                    wg[:].rearrange("p (q c i j) -> p q c j i", q=2, i=4, j=4),
+                    src.rearrange("p q j (c i) -> p q c j i", i=4),
+                )
+            else:
+                interleave(W2_ENGINE[2 * e + g], wg[:], raws["h%d" % e][:, g * 1024 : (g + 1) * 1024])
             w2g[2 * e + g] = wg
             was_read("h%d" % e)
 
@@ -210,23 +219,23 @@ def tile_routed_moe_kernel(tc, xT, w1, w2, gate, offs, pos1, pos2, out):
             w2s[h] = keep.tile([P, N], U8, name="w2s%d" % h, align_bytes=64)
             nc.vector.quantize_mx(out=w2c[h][:].bitcast(FP8X4), scales=w2s[h][:], in_=w2g[h][:])
 
-        def layer2(e):
-            accs = []
-            for b in range(2):
+        def layer2(e, blocks):
+            accs = {}
+            for b in blocks:
                 acc = ps2.tile([P, C], F32, name="acc2", tag="acc2")
-                accs.append(acc)
-                wcols = slice(b * 128, (b + 1) * 128)
+                accs[b] = acc
                 for g in range(2):
+                    which, wcols = (b, slice(g * 128, (g + 1) * 128)) if e in BY_BLOCK else (g, slice(b * 128, (b + 1) * 128))
                     nc.tensor.matmul_mx(
                         out=acc[:],
-                        lhsT=w2c[2 * e + g][:, wcols].bitcast(FP8X4),
-                        lhsT_scale=w2s[2 * e + g][:, wcols],
+                        lhsT=w2c[2 * e + which][:, wcols].bitcast(FP8X4),
+                        lhsT_scale=w2s[2 * e + which][:, wcols],
                         rhs=hc[2 * e + g][:].bitcast(FP8X4),
                         rhs_scale=hs[2 * e + g][:],
                         start=(g == 0),
                         stop=(g == 1),
                     )
-            for b in range(2):
+            for b in blocks:
                 copy_on(Y_ENGINE[2 * e + b], y[b][:, e * C : (e + 1) * C], accs[b][:])
 
         pending = []
@@ -234,9 +243,15 @@ def tile_routed_moe_kernel(tc, xT, w1, w2, gate, offs, pos1, pos2, out):
 
         def second_layers():
             for e in range(E):
-                if e not in done2 and 2 * e + 1 in w2c and 2 * e + 1 in hc:
-                    layer2(e)
-                    done2.append(e)
+                if 2 * e + 1 not in hc:
+                    continue
+                if e in BY_BLOCK:
+                    blocks = [b for b in range(2) if (e, b) not in done2 and 2 * e + b in w2c]
+                else:
+                    blocks = [b for b in range(2) if (e, b) not in done2 and 2 * e + 1 in w2c]
+                if blocks:
+                    layer2(e, blocks)
+                    done2.extend((e, b) for b in blocks)
 
         def hidden_quants():
             for k in pending:
@@ -274,12 +289,19 @@ def tile_routed_moe_kernel(tc, xT, w1, w2, gate, offs, pos1, pos2, out):
                         pending.append(2 * e + g)
             elif name[0] == "h":
                 e = int(name[1])
-                for g in range(2):
-                    w2_copy(e, g)
-                hidden_quants()
-                for g in range(2):
-                    w2_quant(2 * e + g)
-                second_layers()
+                if e in BY_BLOCK:
+                    hidden_quants()
+                    for b in range(2):
+                        w2_copy(e, b)
+                        w2_quant(2 * e + b)
+                        second_layers()
+                else:
+                    for g in range(2):
+                        w2_copy(e, g)
+                    hidden_quants()
+                    for g in range(2):
+                        w2_quant(2 * e + g)
+                    second_layers()
         hidden_quants()
 
         graw = raws["gate"]

@@ -23,10 +23,9 @@ DEPTH = 6
 ORDER = ["x0","x1","w00","w01","w10","w11","w20","w21","w30","w31","h0","h1","h2","h3","gate"]
 X_ENGINE = "vs"
 W1_ENGINE = "sssvvvsvvvsvvvvs"
-W2_ENGINE = "vvvsvvvv"
-Y_ENGINE = "ssssssvs"
-IN_HALVES = [2]
-BY_BLOCK = [3]
+W2_ENGINE = "vsvsvsvv"
+Y_ENGINE = "ssssssss"
+IN_HALVES = []
 
 
 def tile_routed_moe_kernel(tc, xT, w1, w2, gate, offs, pos1, pos2, out):
@@ -197,27 +196,39 @@ def tile_routed_moe_kernel(tc, xT, w1, w2, gate, offs, pos1, pos2, out):
 
         y = [keep.tile([P, E * C], F32, name="y%d" % b) for b in range(2)]
         w2g = {}
+        late = keep.tile([P, E * 1024], BF16, name="late", align_bytes=64)
         w2c = {}
         w2s = {}
 
         def w2_copy(e, g):
-            wg = grp.tile([P, CHUNK // 2], BF16, name="wg2", tag="grp", align_bytes=64)
-            if e in BY_BLOCK:
-                src = raws["h%d" % e][:].rearrange("p (q j n) -> p q j n", q=2, j=4)[:, :, :, g * 128 : (g + 1) * 128]
-                copy_on(
-                    W2_ENGINE[2 * e + g],
-                    wg[:].rearrange("p (q c i j) -> p q c j i", q=2, i=4, j=4),
-                    src.rearrange("p q j (c i) -> p q c j i", i=4),
-                )
+            if g == 0:
+                wg = grp.tile([P, CHUNK // 2], BF16, name="wg2", tag="grp", align_bytes=64)
+                w2g[e] = wg
+                dst = wg[:]
             else:
-                interleave(W2_ENGINE[2 * e + g], wg[:], raws["h%d" % e][:, g * 1024 : (g + 1) * 1024])
-            w2g[2 * e + g] = wg
+                dst = late[:, e * 1024 : (e + 1) * 1024]
+            src = raws["h%d" % e][:].rearrange("p (q j n) -> p q j n", q=2, j=4)[:, :, :, g * 128 : (g + 1) * 128]
+            copy_on(
+                W2_ENGINE[2 * e + g],
+                dst.rearrange("p (q c i j) -> p q c j i", q=2, i=4, j=4),
+                src.rearrange("p q j (c i) -> p q c j i", i=4),
+            )
             was_read("h%d" % e)
 
-        def w2_quant(h):
-            w2c[h] = keep.tile([P, N], U32, name="w2c%d" % h, align_bytes=64)
-            w2s[h] = keep.tile([P, N], U8, name="w2s%d" % h, align_bytes=64)
-            nc.vector.quantize_mx(out=w2c[h][:].bitcast(FP8X4), scales=w2s[h][:], in_=w2g[h][:])
+        def w2_quant(e):
+            codes = keep.tile([P, N], U32, name="w2c%d" % e, align_bytes=64)
+            scales = keep.tile([P, N], U8, name="w2s%d" % e, align_bytes=64)
+            nc.vector.quantize_mx(out=codes[:].bitcast(FP8X4), scales=scales[:], in_=w2g[e][:])
+            w2c[(e, 0)] = codes[:]
+            w2s[(e, 0)] = scales[:]
+
+        def w2_quant_late():
+            codes = keep.tile([P, E * N], U32, name="w2c_late", align_bytes=64)
+            scales = keep.tile([P, E * N], U8, name="w2s_late", align_bytes=64)
+            nc.vector.quantize_mx(out=codes[:].bitcast(FP8X4), scales=scales[:], in_=late[:])
+            for e in range(E):
+                w2c[(e, 1)] = codes[:, e * N : (e + 1) * N]
+                w2s[(e, 1)] = scales[:, e * N : (e + 1) * N]
 
         def layer2(e, blocks):
             accs = {}
@@ -225,11 +236,11 @@ def tile_routed_moe_kernel(tc, xT, w1, w2, gate, offs, pos1, pos2, out):
                 acc = ps2.tile([P, C], F32, name="acc2", tag="acc2")
                 accs[b] = acc
                 for g in range(2):
-                    which, wcols = (b, slice(g * 128, (g + 1) * 128)) if e in BY_BLOCK else (g, slice(b * 128, (b + 1) * 128))
+                    wcols = slice(g * 128, (g + 1) * 128)
                     nc.tensor.matmul_mx(
                         out=acc[:],
-                        lhsT=w2c[2 * e + which][:, wcols].bitcast(FP8X4),
-                        lhsT_scale=w2s[2 * e + which][:, wcols],
+                        lhsT=w2c[(e, b)][:, wcols].bitcast(FP8X4),
+                        lhsT_scale=w2s[(e, b)][:, wcols],
                         rhs=hc[2 * e + g][:].bitcast(FP8X4),
                         rhs_scale=hs[2 * e + g][:],
                         start=(g == 0),
@@ -245,10 +256,7 @@ def tile_routed_moe_kernel(tc, xT, w1, w2, gate, offs, pos1, pos2, out):
             for e in range(E):
                 if 2 * e + 1 not in hc:
                     continue
-                if e in BY_BLOCK:
-                    blocks = [b for b in range(2) if (e, b) not in done2 and 2 * e + b in w2c]
-                else:
-                    blocks = [b for b in range(2) if (e, b) not in done2 and 2 * e + 1 in w2c]
+                blocks = [b for b in range(2) if (e, b) not in done2 and (e, b) in w2c]
                 if blocks:
                     layer2(e, blocks)
                     done2.extend((e, b) for b in blocks)
@@ -289,18 +297,13 @@ def tile_routed_moe_kernel(tc, xT, w1, w2, gate, offs, pos1, pos2, out):
                         pending.append(2 * e + g)
             elif name[0] == "h":
                 e = int(name[1])
-                if e in BY_BLOCK:
-                    hidden_quants()
-                    for b in range(2):
-                        w2_copy(e, b)
-                        w2_quant(2 * e + b)
-                        second_layers()
-                else:
-                    for g in range(2):
-                        w2_copy(e, g)
-                    hidden_quants()
-                    for g in range(2):
-                        w2_quant(2 * e + g)
+                hidden_quants()
+                w2_copy(e, 0)
+                w2_quant(e)
+                second_layers()
+                w2_copy(e, 1)
+                if e == E - 1:
+                    w2_quant_late()
                     second_layers()
         hidden_quants()
 

@@ -81,6 +81,8 @@ def tile_routed_moe_kernel(tc, xT, w1, w2, gate, offs, pos1, pos2, out):
                     dma(out=raw[:].rearrange("p (g c) -> p g c", g=2), in_=w2_v[:, e])
             else:
                 dma(out=raw[:].rearrange("p (r b t) -> p r b t", r=2, b=2), in_=gate_v)
+                dma(pos1_t[:], pos1)
+                dma(pos2_t[:], pos2)
             raws[name] = raw
             return True
 
@@ -285,9 +287,6 @@ def tile_routed_moe_kernel(tc, xT, w1, w2, gate, offs, pos1, pos2, out):
                     w1_copy(e, s, g)
                 if name == "w00":
                     gather(1, 3)
-                if name == "w10":
-                    nc.sync.dma_start(pos1_t[:], pos1)
-                    nc.sync.dma_start(pos2_t[:], pos2)
                 for g in range(2):
                     w1_quant(e, s, g)
                 hidden_quants()

@@ -1,6 +1,7 @@
 from contextlib import ExitStack
 
 import concourse.mybir as mybir
+from concourse.masks import make_identity
 
 K, T, E, C, H, N = 1024, 512, 4, 256, 1024, 256
 FLOPS = 2 * E * C * (K * H + H * N)
@@ -124,6 +125,8 @@ def tile_routed_moe_kernel(tc, xT, w1, w2, gate, offs, pos1, pos2, out):
         warm2 = keep.tile([P, 1], F32, name="warm2")
         nc.vector.memset(warm[:], 0.0)
         nc.scalar.activation(out=warm2[:], in_=warm[:], func=GELU)
+        ident = keep.tile([P, P], F32, name="ident")
+        make_identity(nc, ident[:])
 
         xw = [keep.tile([P, 2 * T], I32, name="xw%d" % s, align_bytes=64) for s in range(2)]
         xs = keep.tile([P, 2 * T], U8, name="xs", align_bytes=64)
@@ -315,5 +318,11 @@ def tile_routed_moe_kernel(tc, xT, w1, w2, gate, offs, pos1, pos2, out):
             nc.vector.tensor_tensor(
                 out=a2[:], in0=y[b][:].indirect(pos2_t[:]), in1=graw[:, (2 + b) * T : (3 + b) * T], op=MULT
             )
-            nc.vector.tensor_tensor(out=res[:], in0=a1[:], in1=a2[:], op=ADD)
+            if b == 0:
+                total = ps1.tile([P, T], F32, name="total", tag="acc1")
+                nc.tensor.matmul(out=total[:], lhsT=ident[:], rhs=a1[:], start=True, stop=False)
+                nc.tensor.matmul(out=total[:], lhsT=ident[:], rhs=a2[:], start=False, stop=True)
+                nc.scalar.copy(out=res[:], in_=total[:])
+            else:
+                nc.vector.tensor_tensor(out=res[:], in0=a1[:], in1=a2[:], op=ADD)
             nc.sync.dma_start(out=out[b * P : (b + 1) * P, :], in_=res[:])

@@ -26,7 +26,7 @@ X_ENGINE = "vs"
 W1_ENGINE = "sssvvvsvvvsvvvvs"
 W2_ENGINE = "vsvsvsvv"
 Y_ENGINE = "ssssssss"
-IN_HALVES = []
+IN_HALVES = [3]
 
 
 def tile_routed_moe_kernel(tc, xT, w1, w2, gate, offs, pos1, pos2, out):
@@ -171,8 +171,14 @@ def tile_routed_moe_kernel(tc, xT, w1, w2, gate, offs, pos1, pos2, out):
             nc.vector.quantize_mx(out=w1c[c][:].bitcast(FP8X4), scales=w1s[c][:], in_=wgs[c][:])
 
         def layer1(e, g):
-            hb = hid.tile([P, 4 * C], BF16, name="hb", tag="hb", align_bytes=64)
-            hbs[2 * e + g] = hb
+            if e == E - 1:
+                if g == 0:
+                    hbs["last"] = keep.tile([P, 8 * C], BF16, name="hb_last", align_bytes=64)
+                hb = hbs["last"][:, g * 4 * C : (g + 1) * 4 * C]
+            else:
+                hbt = hid.tile([P, 4 * C], BF16, name="hb", tag="hb", align_bytes=64)
+                hbs[2 * e + g] = hbt
+                hb = hbt[:]
             for half in range(2):
                 cols = slice(half * 128, (half + 1) * 128)
                 acc = ps1.tile([P, 4, 128], F32, name="acc1", tag="acc1")
@@ -195,9 +201,21 @@ def tile_routed_moe_kernel(tc, xT, w1, w2, gate, offs, pos1, pos2, out):
                 )
 
         def h_quant(k):
-            hc[k] = keep.tile([P, C], U32, name="hc%d" % k, align_bytes=64)
-            hs[k] = keep.tile([P, C], U8, name="hs%d" % k, align_bytes=64)
-            nc.vector.quantize_mx(out=hc[k][:].bitcast(FP8X4), scales=hs[k][:], in_=hbs[k][:])
+            if k == 2 * E - 2:
+                return
+            if k == 2 * E - 1:
+                codes = keep.tile([P, 2 * C], U32, name="hc_last", align_bytes=64)
+                scales = keep.tile([P, 2 * C], U8, name="hs_last", align_bytes=64)
+                nc.vector.quantize_mx(out=codes[:].bitcast(FP8X4), scales=scales[:], in_=hbs["last"][:])
+                for g in range(2):
+                    hc[k - 1 + g] = codes[:, g * C : (g + 1) * C]
+                    hs[k - 1 + g] = scales[:, g * C : (g + 1) * C]
+                return
+            codes = keep.tile([P, C], U32, name="hc%d" % k, align_bytes=64)
+            scales = keep.tile([P, C], U8, name="hs%d" % k, align_bytes=64)
+            nc.vector.quantize_mx(out=codes[:].bitcast(FP8X4), scales=scales[:], in_=hbs[k][:])
+            hc[k] = codes[:]
+            hs[k] = scales[:]
 
         y = [keep.tile([P, E * C], F32, name="y%d" % b) for b in range(2)]
         w2g = {}
@@ -218,6 +236,18 @@ def tile_routed_moe_kernel(tc, xT, w1, w2, gate, offs, pos1, pos2, out):
                 dst.rearrange("p (q c i j) -> p q c j i", q=2, i=4, j=4),
                 src.rearrange("p q j (c i) -> p q c j i", i=4),
             )
+            was_read("h%d" % e)
+
+        def w2_copy_pass(e, q):
+            if q == 0:
+                w2g[e] = grp.tile([P, CHUNK // 2], BF16, name="wg2", tag="grp", align_bytes=64)
+            for b, whole in ((0, w2g[e][:]), (1, late[:, e * 1024 : (e + 1) * 1024])):
+                src = raws["h%d" % e][:, q * 1024 : (q + 1) * 1024].rearrange("p (j n) -> p j n", j=4)[:, :, b * 128 : (b + 1) * 128]
+                copy_on(
+                    W2_ENGINE[2 * e + b],
+                    whole[:, q * 512 : (q + 1) * 512].rearrange("p (c i j) -> p c j i", i=4, j=4),
+                    src.rearrange("p j (c i) -> p c j i", i=4),
+                )
             was_read("h%d" % e)
 
         def w2_quant(e):
@@ -246,8 +276,8 @@ def tile_routed_moe_kernel(tc, xT, w1, w2, gate, offs, pos1, pos2, out):
                         out=acc[:],
                         lhsT=w2c[(e, b)][:, wcols].bitcast(FP8X4),
                         lhsT_scale=w2s[(e, b)][:, wcols],
-                        rhs=hc[2 * e + g][:].bitcast(FP8X4),
-                        rhs_scale=hs[2 * e + g][:],
+                        rhs=hc[2 * e + g].bitcast(FP8X4),
+                        rhs_scale=hs[2 * e + g],
                         start=(g == 0),
                         stop=(g == 1),
                     )
@@ -300,10 +330,16 @@ def tile_routed_moe_kernel(tc, xT, w1, w2, gate, offs, pos1, pos2, out):
             elif name[0] == "h":
                 e = int(name[1])
                 hidden_quants()
-                w2_copy(e, 0)
-                w2_quant(e)
-                second_layers()
-                w2_copy(e, 1)
+                if e in IN_HALVES:
+                    for q in range(2):
+                        w2_copy_pass(e, q)
+                    w2_quant(e)
+                    second_layers()
+                else:
+                    w2_copy(e, 0)
+                    w2_quant(e)
+                    second_layers()
+                    w2_copy(e, 1)
                 if e == E - 1:
                     w2_quant_late()
                     second_layers()

@@ -81,9 +81,10 @@ def tile_routed_moe_kernel(tc, xT, w1, w2, gate, offs, pos1, pos2, out):
                 else:
                     dma(out=raw[:].rearrange("p (g c) -> p g c", g=2), in_=w2_v[:, e])
             else:
-                dma(out=raw[:].rearrange("p (r b t) -> p r b t", r=2, b=2), in_=gate_v)
                 dma(pos1_t[:], pos1)
                 dma(pos2_t[:], pos2)
+                for b in range(2):
+                    dma(out=raw[:].rearrange("p (r b t) -> p r b t", r=2, b=2)[:, :, b, :], in_=gate_v[:, :, b, :])
             raws[name] = raw
             return True
 
@@ -331,10 +332,23 @@ def tile_routed_moe_kernel(tc, xT, w1, w2, gate, offs, pos1, pos2, out):
                 e = int(name[1])
                 hidden_quants()
                 if e in IN_HALVES:
+                    acc = ps2.tile([P, C], F32, name="acc2", tag="acc2")
                     for q in range(2):
                         w2_copy_pass(e, q)
-                    w2_quant(e)
-                    second_layers()
+                        codes = keep.tile([P, 128], U32, name="w2c%d_%d" % (e, q), align_bytes=64)
+                        scales = keep.tile([P, 128], U8, name="w2s%d_%d" % (e, q), align_bytes=64)
+                        nc.vector.quantize_mx(out=codes[:].bitcast(FP8X4), scales=scales[:], in_=w2g[e][:, q * 512 : (q + 1) * 512])
+                        nc.tensor.matmul_mx(
+                            out=acc[:],
+                            lhsT=codes[:].bitcast(FP8X4),
+                            lhsT_scale=scales[:],
+                            rhs=hc[2 * e + q].bitcast(FP8X4),
+                            rhs_scale=hs[2 * e + q],
+                            start=(q == 0),
+                            stop=(q == 1),
+                        )
+                    copy_on(Y_ENGINE[2 * e], y[0][:, e * C : (e + 1) * C], acc[:])
+                    done2.append((e, 0))
                 else:
                     w2_copy(e, 0)
                     w2_quant(e)

@@ -26,6 +26,7 @@ X_ENGINE = "vs"
 W1_ENGINE = "sssvvvsvvvsvvvvs"
 W2_ENGINE = "vsvsvsvv"
 Y_ENGINE = "ssssssss"
+HIDDEN_HOME = [(1, 1, 1), (2, 1, 1), (3, 0, 1)]
 IN_HALVES = [3]
 
 
@@ -36,7 +37,7 @@ def tile_routed_moe_kernel(tc, xT, w1, w2, gate, offs, pos1, pos2, out):
         keep = ctx.enter_context(tc.tile_pool(name="keep", bufs=1))
         stage = ctx.enter_context(tc.tile_pool(name="stage", bufs=DEPTH))
         grp = ctx.enter_context(tc.tile_pool(name="grp", bufs=4))
-        hid = ctx.enter_context(tc.tile_pool(name="hid", bufs=3))
+        hid = ctx.enter_context(tc.tile_pool(name="hid", bufs=4))
         fin = ctx.enter_context(tc.tile_pool(name="fin", bufs=2))
         ps1 = ctx.enter_context(tc.psum_pool(name="ps1", bufs=4))
         ps2 = ctx.enter_context(tc.psum_pool(name="ps2", bufs=4))
@@ -206,17 +207,18 @@ def tile_routed_moe_kernel(tc, xT, w1, w2, gate, offs, pos1, pos2, out):
                 return
             if k == 2 * E - 1:
                 codes = keep.tile([P, 2 * C], U32, name="hc_last", align_bytes=64)
-                scales = keep.tile([P, 2 * C], U8, name="hs_last", align_bytes=64)
-                nc.vector.quantize_mx(out=codes[:].bitcast(FP8X4), scales=scales[:], in_=hbs["last"][:])
+                home = keep.tile([P, 2 * C], U8, name="hs_last", align_bytes=64)
+                nc.vector.quantize_mx(out=codes[:].bitcast(FP8X4), scales=home[:], in_=hbs["last"][:])
                 for g in range(2):
                     hc[k - 1 + g] = codes[:, g * C : (g + 1) * C]
-                    hs[k - 1 + g] = scales[:, g * C : (g + 1) * C]
+                    hs[k - 1 + g] = home[:, g * C : (g + 1) * C]
                 return
             codes = keep.tile([P, C], U32, name="hc%d" % k, align_bytes=64)
-            scales = keep.tile([P, C], U8, name="hs%d" % k, align_bytes=64)
-            nc.vector.quantize_mx(out=codes[:].bitcast(FP8X4), scales=scales[:], in_=hbs[k][:])
+            e, g = k // 2, k % 2
+            home = w1s[HIDDEN_HOME[e]][4:P, g * C : (g + 1) * C]
+            nc.vector.quantize_mx(out=codes[:].bitcast(FP8X4), scales=home, in_=hbs[k][:])
             hc[k] = codes[:]
-            hs[k] = scales[:]
+            hs[k] = home
 
         y = [keep.tile([P, E * C], F32, name="y%d" % b) for b in range(2)]
         w2g = {}
@@ -285,7 +287,6 @@ def tile_routed_moe_kernel(tc, xT, w1, w2, gate, offs, pos1, pos2, out):
             for b in blocks:
                 copy_on(Y_ENGINE[2 * e + b], y[b][:, e * C : (e + 1) * C], accs[b][:])
 
-        pending = []
         done2 = []
 
         def second_layers():
@@ -297,10 +298,9 @@ def tile_routed_moe_kernel(tc, xT, w1, w2, gate, offs, pos1, pos2, out):
                     layer2(e, blocks)
                     done2.extend((e, b) for b in blocks)
 
-        def hidden_quants():
-            for k in pending:
+        def hidden_quants(ks):
+            for k in ks:
                 h_quant(k)
-            pending.clear()
             second_layers()
 
         xgs = []
@@ -323,14 +323,16 @@ def tile_routed_moe_kernel(tc, xT, w1, w2, gate, offs, pos1, pos2, out):
                     gather(1, 3)
                 for g in range(2):
                     w1_quant(e, s, g)
-                hidden_quants()
+                if (e, s, 1) in HIDDEN_HOME:
+                    k = 2 * HIDDEN_HOME.index((e, s, 1))
+                    hidden_quants([k, k + 1])
                 if s == 1:
                     for g in range(2):
                         layer1(e, g)
-                        pending.append(2 * e + g)
             elif name[0] == "h":
                 e = int(name[1])
-                hidden_quants()
+                if e == 0:
+                    hidden_quants([6, 7])
                 if e in IN_HALVES:
                     acc = ps2.tile([P, C], F32, name="acc2", tag="acc2")
                     for q in range(2):
@@ -357,7 +359,6 @@ def tile_routed_moe_kernel(tc, xT, w1, w2, gate, offs, pos1, pos2, out):
                 if e == E - 1:
                     w2_quant_late()
                     second_layers()
-        hidden_quants()
 
         graw = raws["gate"]
         for b in range(2):

@@ -24,8 +24,7 @@ DEPTH = 6
 ORDER = ["x0","x1","w00","w01","w10","w11","w20","w21","w30","w31","h0","h1","h2","h3","gate"]
 X_ENGINE = "vs"
 W1_ENGINE = "sssvvvsvvvsvvvvs"
-W2_ENGINE = "vsvsvsvv"
-Y_ENGINE = "ssssssss"
+W2_ENGINE = "vsvvvsvs"
 HIDDEN_HOME = [(1, 1, 1), (2, 1, 1), (3, 0, 1)]
 IN_HALVES = [3]
 
@@ -85,7 +84,7 @@ def tile_routed_moe_kernel(tc, xT, w1, w2, gate, offs, pos1, pos2, out):
                 dma(pos1_t[:], pos1)
                 dma(pos2_t[:], pos2)
                 for b in range(2):
-                    dma(out=raw[:].rearrange("p (r b t) -> p r b t", r=2, b=2)[:, :, b, :], in_=gate_v[:, :, b, :])
+                    dma(out=raw[:, 2 * b * T : 2 * (b + 1) * T].rearrange("p (r t) -> p r t", r=2), in_=gate_v[:, :, b, :])
             raws[name] = raw
             return True
 
@@ -202,13 +201,15 @@ def tile_routed_moe_kernel(tc, xT, w1, w2, gate, offs, pos1, pos2, out):
                     func=GELU,
                 )
 
+        late_scales = {}
+
         def h_quant(k):
             if k == 2 * E - 2:
                 return
             if k == 2 * E - 1:
                 codes = keep.tile([P, 2 * C], U32, name="hc_last", align_bytes=64)
-                home = keep.tile([P, 2 * C], U8, name="hs_last", align_bytes=64)
-                nc.vector.quantize_mx(out=codes[:].bitcast(FP8X4), scales=home[:], in_=hbs["last"][:])
+                home = late_scales[0][4:P, :]
+                nc.vector.quantize_mx(out=codes[:].bitcast(FP8X4), scales=home, in_=hbs["last"][:])
                 for g in range(2):
                     hc[k - 1 + g] = codes[:, g * C : (g + 1) * C]
                     hs[k - 1 + g] = home[:, g * C : (g + 1) * C]
@@ -222,9 +223,12 @@ def tile_routed_moe_kernel(tc, xT, w1, w2, gate, offs, pos1, pos2, out):
 
         y = [keep.tile([P, E * C], F32, name="y%d" % b) for b in range(2)]
         w2g = {}
-        late = keep.tile([P, E * 1024], BF16, name="late", align_bytes=64)
+        late = [keep.tile([P, 2 * 1024], BF16, name="late%d" % i, align_bytes=64) for i in range(2)]
         w2c = {}
         w2s = {}
+
+        def late_of(e):
+            return late[e // 2][:, (e % 2) * 1024 : (e % 2 + 1) * 1024]
 
         def w2_copy(e, g):
             if g == 0:
@@ -232,7 +236,7 @@ def tile_routed_moe_kernel(tc, xT, w1, w2, gate, offs, pos1, pos2, out):
                 w2g[e] = wg
                 dst = wg[:]
             else:
-                dst = late[:, e * 1024 : (e + 1) * 1024]
+                dst = late_of(e)
             src = raws["h%d" % e][:].rearrange("p (q j n) -> p q j n", q=2, j=4)[:, :, :, g * 128 : (g + 1) * 128]
             copy_on(
                 W2_ENGINE[2 * e + g],
@@ -241,17 +245,16 @@ def tile_routed_moe_kernel(tc, xT, w1, w2, gate, offs, pos1, pos2, out):
             )
             was_read("h%d" % e)
 
-        def w2_copy_pass(e, q):
-            if q == 0:
+        def w2_copy_pass(e, q, b):
+            if q == 0 and b == 0:
                 w2g[e] = grp.tile([P, CHUNK // 2], BF16, name="wg2", tag="grp", align_bytes=64)
-            for b, whole in ((0, w2g[e][:]), (1, late[:, e * 1024 : (e + 1) * 1024])):
-                src = raws["h%d" % e][:, q * 1024 : (q + 1) * 1024].rearrange("p (j n) -> p j n", j=4)[:, :, b * 128 : (b + 1) * 128]
-                copy_on(
-                    W2_ENGINE[2 * e + b],
-                    whole[:, q * 512 : (q + 1) * 512].rearrange("p (c i j) -> p c j i", i=4, j=4),
-                    src.rearrange("p j (c i) -> p c j i", i=4),
-                )
-            was_read("h%d" % e)
+            whole = w2g[e][:] if b == 0 else late_of(e)
+            src = raws["h%d" % e][:, q * 1024 : (q + 1) * 1024].rearrange("p (j n) -> p j n", j=4)[:, :, b * 128 : (b + 1) * 128]
+            copy_on(
+                W2_ENGINE[2 * e + b],
+                whole[:, q * 512 : (q + 1) * 512].rearrange("p (c i j) -> p c j i", i=4, j=4),
+                src.rearrange("p j (c i) -> p c j i", i=4),
+            )
 
         def w2_quant(e):
             codes = keep.tile([P, N], U32, name="w2c%d" % e, align_bytes=64)
@@ -260,48 +263,34 @@ def tile_routed_moe_kernel(tc, xT, w1, w2, gate, offs, pos1, pos2, out):
             w2c[(e, 0)] = codes[:]
             w2s[(e, 0)] = scales[:]
 
-        def w2_quant_late():
-            codes = keep.tile([P, E * N], U32, name="w2c_late", align_bytes=64)
-            scales = keep.tile([P, E * N], U8, name="w2s_late", align_bytes=64)
-            nc.vector.quantize_mx(out=codes[:].bitcast(FP8X4), scales=scales[:], in_=late[:])
-            for e in range(E):
-                w2c[(e, 1)] = codes[:, e * N : (e + 1) * N]
-                w2s[(e, 1)] = scales[:, e * N : (e + 1) * N]
+        def w2_quant_late(i):
+            codes = keep.tile([P, 2 * N], U32, name="w2c_late%d" % i, align_bytes=64)
+            scales = keep.tile([P, 2 * N], U8, name="w2s_late%d" % i, align_bytes=64)
+            late_scales[i] = scales
+            nc.vector.quantize_mx(out=codes[:].bitcast(FP8X4), scales=scales[:], in_=late[i][:])
+            for j in range(2):
+                w2c[(2 * i + j, 1)] = codes[:, j * N : (j + 1) * N]
+                w2s[(2 * i + j, 1)] = scales[:, j * N : (j + 1) * N]
 
-        def layer2(e, blocks):
-            accs = {}
-            for b in blocks:
-                acc = ps2.tile([P, C], F32, name="acc2", tag="acc2")
-                accs[b] = acc
-                for g in range(2):
-                    wcols = slice(g * 128, (g + 1) * 128)
-                    nc.tensor.matmul_mx(
-                        out=acc[:],
-                        lhsT=w2c[(e, b)][:, wcols].bitcast(FP8X4),
-                        lhsT_scale=w2s[(e, b)][:, wcols],
-                        rhs=hc[2 * e + g].bitcast(FP8X4),
-                        rhs_scale=hs[2 * e + g],
-                        start=(g == 0),
-                        stop=(g == 1),
-                    )
-            for b in blocks:
-                copy_on(Y_ENGINE[2 * e + b], y[b][:, e * C : (e + 1) * C], accs[b][:])
+        def layer2(e, b, acc):
+            for g in range(2):
+                wcols = slice(g * 128, (g + 1) * 128)
+                nc.tensor.matmul_mx(
+                    out=acc,
+                    lhsT=w2c[(e, b)][:, wcols].bitcast(FP8X4),
+                    lhsT_scale=w2s[(e, b)][:, wcols],
+                    rhs=hc[2 * e + g].bitcast(FP8X4),
+                    rhs_scale=hs[2 * e + g],
+                    start=(g == 0),
+                    stop=(g == 1),
+                )
 
-        done2 = []
-
-        def second_layers():
-            for e in range(E):
-                if 2 * e + 1 not in hc:
-                    continue
-                blocks = [b for b in range(2) if (e, b) not in done2 and (e, b) in w2c]
-                if blocks:
-                    layer2(e, blocks)
-                    done2.extend((e, b) for b in blocks)
+        def sums(name):
+            return ps2.tile([P, 2 * C], F32, name=name, tag="acc2")
 
         def hidden_quants(ks):
             for k in ks:
                 h_quant(k)
-            second_layers()
 
         xgs = []
         for name in ORDER:
@@ -331,17 +320,36 @@ def tile_routed_moe_kernel(tc, xT, w1, w2, gate, offs, pos1, pos2, out):
                         layer1(e, g)
             elif name[0] == "h":
                 e = int(name[1])
-                if e == 0:
-                    hidden_quants([6, 7])
-                if e in IN_HALVES:
-                    acc = ps2.tile([P, C], F32, name="acc2", tag="acc2")
+                if e < E - 1:
+                    w2_copy(e, 0)
+                    w2_quant(e)
+                    if e == 0:
+                        first = sums("first")
+                    if e < 2:
+                        layer2(e, 0, first[:, e * C : (e + 1) * C])
+                    w2_copy(e, 1)
+                    if e == 1:
+                        nc.scalar.copy(out=y[0][:, 0 : 2 * C], in_=first[:])
+                        w2_quant_late(0)
+                        hidden_quants([6, 7])
+                        pairs = [sums("pair%d" % j) for j in range(2)]
+                        for j in range(2):
+                            layer2(j, 1, pairs[j][:, 0:C])
+                    if e == 2:
+                        third = sums("third")
+                        layer2(e, 0, third[:, 0:C])
+                        nc.scalar.copy(out=y[0][:, 2 * C : 3 * C], in_=third[:, 0:C])
+                else:
+                    last = sums("last")
                     for q in range(2):
-                        w2_copy_pass(e, q)
+                        for b in range(2):
+                            w2_copy_pass(e, q, b)
+                        was_read("h%d" % e)
                         codes = keep.tile([P, 128], U32, name="w2c%d_%d" % (e, q), align_bytes=64)
                         scales = keep.tile([P, 128], U8, name="w2s%d_%d" % (e, q), align_bytes=64)
                         nc.vector.quantize_mx(out=codes[:].bitcast(FP8X4), scales=scales[:], in_=w2g[e][:, q * 512 : (q + 1) * 512])
                         nc.tensor.matmul_mx(
-                            out=acc[:],
+                            out=last[:, 0:C],
                             lhsT=codes[:].bitcast(FP8X4),
                             lhsT_scale=scales[:],
                             rhs=hc[2 * e + q].bitcast(FP8X4),
@@ -349,25 +357,23 @@ def tile_routed_moe_kernel(tc, xT, w1, w2, gate, offs, pos1, pos2, out):
                             start=(q == 0),
                             stop=(q == 1),
                         )
-                    copy_on(Y_ENGINE[2 * e], y[0][:, e * C : (e + 1) * C], acc[:])
-                    done2.append((e, 0))
-                else:
-                    w2_copy(e, 0)
-                    w2_quant(e)
-                    second_layers()
-                    w2_copy(e, 1)
-                if e == E - 1:
-                    w2_quant_late()
-                    second_layers()
+                    nc.scalar.copy(out=y[0][:, e * C : (e + 1) * C], in_=last[:, 0:C])
+                    w2_quant_late(1)
+                    for j in range(2):
+                        layer2(2 + j, 1, pairs[j][:, C : 2 * C])
+                        nc.scalar.copy(
+                            out=y[1][:].rearrange("p (u j c) -> p j u c", u=2, j=2)[:, j],
+                            in_=pairs[j][:].rearrange("p (u c) -> p u c", u=2),
+                        )
 
         graw = raws["gate"]
         for b in range(2):
             a1 = fin.tile([P, T], F32, name="a1", tag="a1")
             a2 = fin.tile([P, T], F32, name="a2", tag="a2")
             res = fin.tile([P, T], F32, name="res", tag="res")
-            nc.vector.tensor_tensor(out=a1[:], in0=y[b][:].indirect(pos1_t[:]), in1=graw[:, b * T : (b + 1) * T], op=MULT)
+            nc.vector.tensor_tensor(out=a1[:], in0=y[b][:].indirect(pos1_t[:]), in1=graw[:, 2 * b * T : (2 * b + 1) * T], op=MULT)
             nc.vector.tensor_tensor(
-                out=a2[:], in0=y[b][:].indirect(pos2_t[:]), in1=graw[:, (2 + b) * T : (3 + b) * T], op=MULT
+                out=a2[:], in0=y[b][:].indirect(pos2_t[:]), in1=graw[:, (2 * b + 1) * T : (2 * b + 2) * T], op=MULT
             )
             if b == 0:
                 total = ps1.tile([P, T], F32, name="total", tag="acc1")

@@ -84,7 +84,8 @@ def tile_routed_moe_kernel(tc, xT, w1, w2, gate, offs, pos1, pos2, out):
                 dma(pos1_t[:], pos1)
                 dma(pos2_t[:], pos2)
                 for b in range(2):
-                    dma(out=raw[:, 2 * b * T : 2 * (b + 1) * T].rearrange("p (r t) -> p r t", r=2), in_=gate_v[:, :, b, :])
+                    for r in range(2):
+                        dma(out=raw[:, (2 * b + r) * T : (2 * b + r + 1) * T], in_=gate_v[:, r, b, :])
             raws[name] = raw
             return True
 

from contextlib import ExitStack

import concourse.mybir as mybir
from concourse.masks import make_identity

K, T, E, C, H, N = 1024, 512, 4, 256, 1024, 256
FLOPS = 2 * E * C * (K * H + H * N)

F32 = mybir.dt.float32
BF16 = mybir.dt.bfloat16
I32 = mybir.dt.int32
U32 = mybir.dt.uint32
U16 = mybir.dt.uint16
U8 = mybir.dt.uint8
FP8X4 = mybir.dt.float8_e4m3fn_x4
GELU = mybir.ActivationFunctionType.Gelu_apprx_tanh
MULT = mybir.AluOpType.mult
ADD = mybir.AluOpType.add

P = 128
CHUNK = 2048
SLOT = 2 * CHUNK
DEPTH = 6
ORDER = ["x0","x1","w00","w01","w10","w11","w20","w21","w30","w31","h0","h1","h2","h3","gate"]
X_ENGINE = "vs"
W1_ENGINE = "sssvvvsvvvsvvvvs"
W2_ENGINE = "vsvvvsvs"
HIDDEN_HOME = [(1, 1, 1), (2, 1, 1), (3, 0, 1)]
IN_HALVES = [3]


def tile_routed_moe_kernel(tc, xT, w1, w2, gate, offs, pos1, pos2, out):
    nc = tc.nc
    with ExitStack() as ctx:
        lists = ctx.enter_context(tc.tile_pool(name="lists", bufs=1))
        keep = ctx.enter_context(tc.tile_pool(name="keep", bufs=1))
        stage = ctx.enter_context(tc.tile_pool(name="stage", bufs=DEPTH))
        grp = ctx.enter_context(tc.tile_pool(name="grp", bufs=4))
        hid = ctx.enter_context(tc.tile_pool(name="hid", bufs=4))
        fin = ctx.enter_context(tc.tile_pool(name="fin", bufs=2))
        ps1 = ctx.enter_context(tc.psum_pool(name="ps1", bufs=4))
        ps2 = ctx.enter_context(tc.psum_pool(name="ps2", bufs=4))

        offs_t = lists.tile([P, E * C // 16], U16, name="offs_t")
        pos1_t = lists.tile([P, T // 16], U16, name="pos1_t")
        pos2_t = lists.tile([P, T // 16], U16, name="pos2_t")
        nc.sync.dma_start(offs_t[:], offs)

        xT_v = xT.rearrange("(s p j) t -> s p j t", p=P, j=4)
        w1_v = w1.rearrange("e (s p j) h -> e s p j h", p=P, j=4)
        w2_v = w2.rearrange("e (g p j) n -> p e g (j n)", p=P, j=4)
        gate_v = gate.rearrange("r (b p) t -> p r b t", p=P)

        issued = [0]
        reads = {}
        raws = {}

        def readers_of(name):
            return 1 if name[0] == "x" else 2

        def load():
            i = issued[0]
            if i >= len(ORDER):
                return False
            if i >= DEPTH and reads.get(ORDER[i - DEPTH], 0) < readers_of(ORDER[i - DEPTH]):
                return False
            name = ORDER[i]
            issued[0] += 1
            dma = nc.sync.dma_start
            width = SLOT if name[0] == "w" else CHUNK
            raw = stage.tile([P, width], F32, name="raw", tag="raw")
            if name[0] == "x":
                dma(out=raw[:].rearrange("p (j t) -> p j t", j=4), in_=xT_v[int(name[1])])
            elif name[0] == "w":
                dma(out=raw[:].rearrange("p (j h) -> p j h", j=4), in_=w1_v[int(name[1]), int(name[2])])
            elif name[0] == "h":
                e = int(name[1])
                if e in IN_HALVES:
                    for g in range(2):
                        dma(out=raw[:, g * 1024 : (g + 1) * 1024], in_=w2_v[:, e, g])
                else:
                    dma(out=raw[:].rearrange("p (g c) -> p g c", g=2), in_=w2_v[:, e])
            else:
                dma(pos1_t[:], pos1)
                dma(pos2_t[:], pos2)
                for b in range(2):
                    for r in range(2):
                        dma(out=raw[:, (2 * b + r) * T : (2 * b + r + 1) * T], in_=gate_v[:, r, b, :])
            raws[name] = raw
            return True

        def pump():
            while load():
                pass

        def was_read(name):
            reads[name] = reads.get(name, 0) + 1
            pump()

        def copy_on(eng, dst, src):
            if eng == "v":
                nc.vector.tensor_copy(out=dst, in_=src)
            else:
                nc.scalar.copy(out=dst, in_=src)

        def interleave(eng, dst, src):
            copy_on(
                eng,
                dst.rearrange("p (c i j) -> p c j i", i=4, j=4),
                src.rearrange("p (j c i) -> p c j i", j=4, i=4),
            )

        def interleave_permuted(eng, dst, src):
            if eng == "v":
                nc.vector.tensor_copy(
                    out=dst.rearrange("p (u v m j) -> p u m j v", u=2, v=2, j=4),
                    in_=src.rearrange("p j (m u v) -> p u m j v", u=2, v=2),
                )
            else:
                nc.scalar.copy(
                    out=dst.rearrange("p (t m j) -> p m j t", t=4, j=4),
                    in_=src.rearrange("p j (m t) -> p m j t", t=4),
                )

        pump()
        warm = keep.tile([P, 1], F32, name="warm")
        warm2 = keep.tile([P, 1], F32, name="warm2")
        nc.vector.memset(warm[:], 0.0)
        nc.scalar.activation(out=warm2[:], in_=warm[:], func=GELU)
        ident = keep.tile([P, P], F32, name="ident")
        make_identity(nc, ident[:])

        xw = [keep.tile([P, 2 * T], I32, name="xw%d" % s, align_bytes=64) for s in range(2)]
        xs = keep.tile([P, 2 * T], U8, name="xs", align_bytes=64)
        for s in range(2):
            nc.vector.memset(xw[s][:, T : 2 * T], 0)
        nc.gpsimd.memset(xs[:], 0)

        gw = {}
        gs = {}

        def gather(first, count):
            sl = offs_t[:, first * (C // 16) : (first + count) * (C // 16)]
            scales = keep.tile([P, count * C], U8, name="gs_%d" % first, align_bytes=64)
            nc.vector.tensor_copy(out=scales[:], in_=xs[:].indirect(sl))
            for s in range(2):
                words = keep.tile([P, count * C], U32, name="gw%d_%d" % (s, first), align_bytes=64)
                nc.vector.tensor_copy(out=words[:], in_=xw[s][:].bitcast(U32).indirect(sl))
                for e in range(first, first + count):
                    part = slice((e - first) * C, (e - first + 1) * C)
                    gw[(s, e)] = words[:, part]
                    gs[(s, e)] = scales[4 * s : P, part]

        w1c = {}
        w1s = {}
        wgs = {}
        hbs = {}
        hc = {}
        hs = {}

        def w1_copy(e, s, g):
            wg = grp.tile([P, CHUNK], BF16, name="wg", tag="grp", align_bytes=64)
            name = "w%d%d" % (e, s)
            src = raws[name][:].rearrange("p (j h) -> p j h", j=4)[:, :, g * 512 : (g + 1) * 512]
            interleave_permuted(W1_ENGINE[4 * e + 2 * s + g], wg[:], src)
            wgs[(e, s, g)] = wg
            was_read(name)

        def w1_quant(e, s, g):
            c = (e, s, g)
            w1c[c] = keep.tile([P, 512], U32, name="w1c%d%d%d" % c, align_bytes=64)
            w1s[c] = keep.tile([P, 512], U8, name="w1s%d%d%d" % c, align_bytes=64)
            nc.vector.quantize_mx(out=w1c[c][:].bitcast(FP8X4), scales=w1s[c][:], in_=wgs[c][:])

        def layer1(e, g):
            if e == E - 1:
                if g == 0:
                    hbs["last"] = keep.tile([P, 8 * C], BF16, name="hb_last", align_bytes=64)
                hb = hbs["last"][:, g * 4 * C : (g + 1) * 4 * C]
            else:
                hbt = hid.tile([P, 4 * C], BF16, name="hb", tag="hb", align_bytes=64)
                hbs[2 * e + g] = hbt
                hb = hbt[:]
            for half in range(2):
                cols = slice(half * 128, (half + 1) * 128)
                acc = ps1.tile([P, 4, 128], F32, name="acc1", tag="acc1")
                for t in range(4):
                    wcols = slice(t * 128, (t + 1) * 128)
                    for s in range(2):
                        nc.tensor.matmul_mx(
                            out=acc[:, t, :],
                            lhsT=w1c[(e, s, g)][:, wcols].bitcast(FP8X4),
                            lhsT_scale=w1s[(e, s, g)][:, wcols],
                            rhs=gw[(s, e)][:, cols].bitcast(FP8X4),
                            rhs_scale=gs[(s, e)][:, cols],
                            start=(s == 0),
                            stop=(s == 1),
                        )
                nc.scalar.activation(
                    out=hb[:, half * 512 : (half + 1) * 512].rearrange("p (n t) -> p n t", t=4),
                    in_=acc[:].rearrange("p t n -> p n t"),
                    func=GELU,
                )

        late_scales = {}

        def h_quant(k):
            if k == 2 * E - 2:
                return
            if k == 2 * E - 1:
                codes = keep.tile([P, 2 * C], U32, name="hc_last", align_bytes=64)
                home = late_scales[0][4:P, :]
                nc.vector.quantize_mx(out=codes[:].bitcast(FP8X4), scales=home, in_=hbs["last"][:])
                for g in range(2):
                    hc[k - 1 + g] = codes[:, g * C : (g + 1) * C]
                    hs[k - 1 + g] = home[:, g * C : (g + 1) * C]
                return
            codes = keep.tile([P, C], U32, name="hc%d" % k, align_bytes=64)
            e, g = k // 2, k % 2
            home = w1s[HIDDEN_HOME[e]][4:P, g * C : (g + 1) * C]
            nc.vector.quantize_mx(out=codes[:].bitcast(FP8X4), scales=home, in_=hbs[k][:])
            hc[k] = codes[:]
            hs[k] = home

        y = [keep.tile([P, E * C], F32, name="y%d" % b) for b in range(2)]
        w2g = {}
        late = [keep.tile([P, 2 * 1024], BF16, name="late%d" % i, align_bytes=64) for i in range(2)]
        w2c = {}
        w2s = {}

        def late_of(e):
            return late[e // 2][:, (e % 2) * 1024 : (e % 2 + 1) * 1024]

        def w2_copy(e, g):
            if g == 0:
                wg = grp.tile([P, CHUNK // 2], BF16, name="wg2", tag="grp", align_bytes=64)
                w2g[e] = wg
                dst = wg[:]
            else:
                dst = late_of(e)
            src = raws["h%d" % e][:].rearrange("p (q j n) -> p q j n", q=2, j=4)[:, :, :, g * 128 : (g + 1) * 128]
            copy_on(
                W2_ENGINE[2 * e + g],
                dst.rearrange("p (q c i j) -> p q c j i", q=2, i=4, j=4),
                src.rearrange("p q j (c i) -> p q c j i", i=4),
            )
            was_read("h%d" % e)

        def w2_copy_pass(e, q, b):
            if q == 0 and b == 0:
                w2g[e] = grp.tile([P, CHUNK // 2], BF16, name="wg2", tag="grp", align_bytes=64)
            whole = w2g[e][:] if b == 0 else late_of(e)
            src = raws["h%d" % e][:, q * 1024 : (q + 1) * 1024].rearrange("p (j n) -> p j n", j=4)[:, :, b * 128 : (b + 1) * 128]
            copy_on(
                W2_ENGINE[2 * e + b],
                whole[:, q * 512 : (q + 1) * 512].rearrange("p (c i j) -> p c j i", i=4, j=4),
                src.rearrange("p j (c i) -> p c j i", i=4),
            )

        def w2_quant(e):
            codes = keep.tile([P, N], U32, name="w2c%d" % e, align_bytes=64)
            scales = keep.tile([P, N], U8, name="w2s%d" % e, align_bytes=64)
            nc.vector.quantize_mx(out=codes[:].bitcast(FP8X4), scales=scales[:], in_=w2g[e][:])
            w2c[(e, 0)] = codes[:]
            w2s[(e, 0)] = scales[:]

        def w2_quant_late(i):
            codes = keep.tile([P, 2 * N], U32, name="w2c_late%d" % i, align_bytes=64)
            scales = keep.tile([P, 2 * N], U8, name="w2s_late%d" % i, align_bytes=64)
            late_scales[i] = scales
            nc.vector.quantize_mx(out=codes[:].bitcast(FP8X4), scales=scales[:], in_=late[i][:])
            for j in range(2):
                w2c[(2 * i + j, 1)] = codes[:, j * N : (j + 1) * N]
                w2s[(2 * i + j, 1)] = scales[:, j * N : (j + 1) * N]

        def layer2(e, b, acc):
            for g in range(2):
                wcols = slice(g * 128, (g + 1) * 128)
                nc.tensor.matmul_mx(
                    out=acc,
                    lhsT=w2c[(e, b)][:, wcols].bitcast(FP8X4),
                    lhsT_scale=w2s[(e, b)][:, wcols],
                    rhs=hc[2 * e + g].bitcast(FP8X4),
                    rhs_scale=hs[2 * e + g],
                    start=(g == 0),
                    stop=(g == 1),
                )

        def sums(name):
            return ps2.tile([P, 2 * C], F32, name=name, tag="acc2")

        def hidden_quants(ks):
            for k in ks:
                h_quant(k)

        xgs = []
        for name in ORDER:
            if name[0] == "x":
                s = int(name[1])
                xg = grp.tile([P, CHUNK], BF16, name="xg", tag="grp", align_bytes=64)
                interleave(X_ENGINE[s], xg[:], raws[name][:])
                was_read(name)
                xgs.append(xg)
                if s == 1:
                    for i in range(2):
                        nc.vector.quantize_mx(out=xw[i][:, 0:T].bitcast(FP8X4), scales=xs[4 * i : P, 0:T], in_=xgs[i][:])
                    gather(0, 1)
            elif name[0] == "w":
                e, s = int(name[1]), int(name[2])
                for g in range(2):
                    w1_copy(e, s, g)
                if name == "w00":
                    gather(1, 3)
                for g in range(2):
                    w1_quant(e, s, g)
                if (e, s, 1) in HIDDEN_HOME:
                    k = 2 * HIDDEN_HOME.index((e, s, 1))
                    hidden_quants([k, k + 1])
                if s == 1:
                    for g in range(2):
                        layer1(e, g)
            elif name[0] == "h":
                e = int(name[1])
                if e < E - 1:
                    w2_copy(e, 0)
                    w2_quant(e)
                    if e == 0:
                        first = sums("first")
                    if e < 2:
                        layer2(e, 0, first[:, e * C : (e + 1) * C])
                    w2_copy(e, 1)
                    if e == 1:
                        nc.scalar.copy(out=y[0][:, 0 : 2 * C], in_=first[:])
                        w2_quant_late(0)
                        hidden_quants([6, 7])
                        pairs = [sums("pair%d" % j) for j in range(2)]
                        for j in range(2):
                            layer2(j, 1, pairs[j][:, 0:C])
                    if e == 2:
                        third = sums("third")
                        layer2(e, 0, third[:, 0:C])
                        nc.scalar.copy(out=y[0][:, 2 * C : 3 * C], in_=third[:, 0:C])
                else:
                    last = sums("last")
                    for q in range(2):
                        for b in range(2):
                            w2_copy_pass(e, q, b)
                        was_read("h%d" % e)
                        codes = keep.tile([P, 128], U32, name="w2c%d_%d" % (e, q), align_bytes=64)
                        scales = keep.tile([P, 128], U8, name="w2s%d_%d" % (e, q), align_bytes=64)
                        nc.vector.quantize_mx(out=codes[:].bitcast(FP8X4), scales=scales[:], in_=w2g[e][:, q * 512 : (q + 1) * 512])
                        nc.tensor.matmul_mx(
                            out=last[:, 0:C],
                            lhsT=codes[:].bitcast(FP8X4),
                            lhsT_scale=scales[:],
                            rhs=hc[2 * e + q].bitcast(FP8X4),
                            rhs_scale=hs[2 * e + q],
                            start=(q == 0),
                            stop=(q == 1),
                        )
                    nc.scalar.copy(out=y[0][:, e * C : (e + 1) * C], in_=last[:, 0:C])
                    w2_quant_late(1)
                    for j in range(2):
                        layer2(2 + j, 1, pairs[j][:, C : 2 * C])
                        nc.scalar.copy(
                            out=y[1][:].rearrange("p (u j c) -> p j u c", u=2, j=2)[:, j],
                            in_=pairs[j][:].rearrange("p (u c) -> p u c", u=2),
                        )

        graw = raws["gate"]
        for b in range(2):
            a1 = fin.tile([P, T], F32, name="a1", tag="a1")
            a2 = fin.tile([P, T], F32, name="a2", tag="a2")
            res = fin.tile([P, T], F32, name="res", tag="res")
            nc.vector.tensor_tensor(out=a1[:], in0=y[b][:].indirect(pos1_t[:]), in1=graw[:, 2 * b * T : (2 * b + 1) * T], op=MULT)
            nc.vector.tensor_tensor(
                out=a2[:], in0=y[b][:].indirect(pos2_t[:]), in1=graw[:, (2 * b + 1) * T : (2 * b + 2) * T], op=MULT
            )
            if b == 0:
                total = ps1.tile([P, T], F32, name="total", tag="acc1")
                nc.tensor.matmul(out=total[:], lhsT=ident[:], rhs=a1[:], start=True, stop=False)
                nc.tensor.matmul(out=total[:], lhsT=ident[:], rhs=a2[:], start=False, stop=True)
                nc.scalar.copy(out=res[:], in_=total[:])
            else:
                nc.vector.tensor_tensor(out=res[:], in0=a1[:], in1=a2[:], op=ADD)
            nc.sync.dma_start(out=out[b * P : (b + 1) * P, :], in_=res[:])
